import numpy as np
import ml_dtypes


def mxq(x, axis, fmt="e4m3"):
    dtype, down = {"e4m3": (ml_dtypes.float8_e4m3fn, 7), "e5m2": (ml_dtypes.float8_e5m2, 14)}[fmt]
    v = np.moveaxis(np.asarray(x, np.float32).astype(ml_dtypes.bfloat16).astype(np.float64), axis, -1)
    blocks = v.reshape(v.shape[:-1] + (-1, 32))
    amax = np.abs(blocks).max(-1, keepdims=True)
    byte = np.maximum(np.where(amax > 0, np.frexp(amax)[1] - 1 + 127, 0) - down, 1)
    scale = np.exp2(byte - 127.0)
    codes = (blocks / scale).astype(np.float32).astype(dtype).astype(np.float64)
    return np.moveaxis((codes * scale).reshape(v.shape), -1, axis)


WIDE = False


def mx_kscale(k):
    if not WIDE:
        return np.ones(k)
    levels = np.array([10, -10, 5, -5, 0])
    if k % 512:
        return np.exp2(np.random.permutation(np.resize(levels, k // 32))).repeat(32)
    a = np.empty((k // 512, 16))
    for p in range(k // 512):
        a[p, :8] = np.random.permutation(np.resize(levels, 8))
        for g in range(8):
            far = levels[np.abs(levels - a[p, g]) >= 10]
            a[p, g + 8] = far[np.random.randint(len(far))]
    return np.exp2(a.ravel()).repeat(32)


def f64(x):
    return np.asarray(x).astype(np.float64)


def striped(idx):
    return np.tile(idx.reshape(-1, 16).T, (8, 1)).astype(np.uint16)


def unstriped(offs):
    return offs[:16].T.reshape(-1).astype(np.int64)

def planes(y):
    n, m = y.shape
    v = y.astype(np.float32).astype(ml_dtypes.bfloat16).astype(np.float64).reshape(n // 32, 32, m)
    top = np.abs(v).max(1)
    byte = np.clip(np.where(top > 0, np.frexp(top)[1] - 1 + 127 - 7, 1), 1, 254)
    codes = (v * np.exp2(127.0 - byte)[:, None, :]).reshape(n, m).astype(np.float32).astype(ml_dtypes.float8_e4m3fn).view(np.uint8)
    words = codes.reshape(n // 512, 128, 4, m).transpose(0, 1, 3, 2)
    return np.ascontiguousarray(words), np.ascontiguousarray(byte.astype(np.uint8).reshape(n // 512, 16, m))


K, T, S, N = 512, 1024, 512, 512
P = 2 ** 7


def setup_inputs():
    n = np.random.standard_normal
    s = mx_kscale(K)[:, None]
    return {
        "xT": (n((K, T)) * s).astype(np.float32),
        "zp": np.tile(np.random.uniform(-0.6, 0.6, T), (P, 1)).astype(np.float32),
        "csum": n((N, 1)).astype(np.float32),
        "w1": (n((K, N)) / np.sqrt(K) / s).astype(np.float32),
        "offs": striped(np.random.permutation(T)[:S]),
    }


def reference(xT, zp, csum, w1, offs):
    xq = mxq(f64(xT)[:, unstriped(offs)], 0, "e4m3")
    y = mxq(f64(w1), 0, "e4m3").T @ xq
    zg = f64(zp)[:1][:, unstriped(offs)]
    out_0 = y - (f64(csum) * zg)
    return (out_0,) + planes(out_0)

@@ -1,0 +1,162 @@
+from contextlib import ExitStack
+
+import concourse.mybir as mybir
+from concourse.masks import make_identity
+
+K, T, S, N = 512, 1024, 512, 512
+FLOPS = 2 * K * S * N
+
+F32 = mybir.dt.float32
+BF16 = mybir.dt.bfloat16
+I32 = mybir.dt.int32
+U32 = mybir.dt.uint32
+U16 = mybir.dt.uint16
+U8 = mybir.dt.uint8
+FP8X4 = mybir.dt.float8_e4m3fn_x4
+MULT = mybir.AluOpType.mult
+ADD = mybir.AluOpType.add
+
+P = 128
+PACK = 4
+HALF = T // 2
+CHUNK = 128
+CHUNKS = S // CHUNK
+
+
+def tile_picked_zeropt_none_lo_kernel(tc, xT, zp, csum, w1, offs, out_0, out_1, out_2):
+    nc = tc.nc
+    with ExitStack() as ctx:
+        keep = ctx.enter_context(tc.tile_pool(name="keep", bufs=1))
+        psum = ctx.enter_context(tc.psum_pool(name="psum", bufs=1))
+
+        x_rows = xT.rearrange("(p j) c -> p j c", j=PACK)
+        w_rows = w1.rearrange("(p j) c -> p j c", j=PACK)
+
+        offsets = keep.tile([P, S // 16], U16, name="offsets")
+        stage = keep.tile([P, 8192], BF16, name="stage", align_bytes=64)
+        w_grouped = stage[:, 0:2048]
+        pairs = [stage[:, 4096:6144], stage[:, 2032:4080]]
+        zp_cols = stage[:, 6128:6144].bitcast(F32)
+        zp_row = stage[:, 6144:8192].bitcast(F32)
+        picked = stage[:, 6144:8192].bitcast(U32).rearrange("p (a n) -> p a n", a=2)
+        csum_cols = keep.tile([P, PACK], F32, name="csum_cols")
+        pieces = [(0, 0, 512), (0, 512, 1024), (1, 0, 384), (1, 384, 768), (1, 768, 1024)]
+        x_raw = [keep.tile([P, 2, hi - lo], F32, name=f"x_raw{i}") for i, (a, lo, hi) in enumerate(pieces)]
+        w_raw = [keep.tile([P, PACK, N // 2], F32, name=f"w_raw{h}") for h in range(2)]
+
+        nc.sync.dma_start(out=zp_cols, in_=zp[0:1, :].rearrange("o (p c) -> (o p) c", c=2 * PACK))
+        nc.scalar.dma_start(out=csum_cols[:], in_=csum.rearrange("(p t) o -> p (t o)", t=PACK))
+        for i, (a, lo, hi) in enumerate(pieces):
+            nc.sync.dma_start(out=x_raw[i][:], in_=x_rows[:, 2 * a:2 * a + 2, lo:hi])
+            if i == 0:
+                nc.sync.dma_start(offsets[:], offs)
+        for h in range(2):
+            nc.sync.dma_start(out=w_raw[h][:], in_=w_rows[:, :, h * (N // 2):(h + 1) * (N // 2)])
+
+        ident = keep.tile([P, P], F32, name="ident")
+        make_identity(nc, ident[:])
+        neg_csum = keep.tile([P, PACK], F32, name="neg_csum")
+        nc.gpsimd.tensor_scalar(neg_csum[:], csum_cols[:], -1.0, 0.0, MULT, ADD)
+
+        for h in range(2):
+            zp_bank = psum.tile([P, PACK, P], F32, name=f"zp_bank{h}")
+            for c in range(PACK):
+                nc.tensor.transpose(zp_bank[:, c, :], zp_cols[:, PACK * h + c:PACK * h + c + 1].to_broadcast([P, P]), ident[:])
+            nc.vector.tensor_copy(
+                out=zp_row.rearrange("p (n h c) -> p h n c", h=2, c=PACK)[:, h, :, :],
+                in_=zp_bank[:].rearrange("p c n -> p n c"))
+
+
+        def cast_pairs(copy, i, lo, hi):
+            a, first, last = pieces[i]
+            copy(out=pairs[a][:, 2 * (first + lo):2 * (first + hi)].rearrange("p (n j) -> p n j", j=2),
+                 in_=x_raw[i][:, :, lo:hi].rearrange("p j n -> p n j"))
+
+        cast_pairs(nc.scalar.copy, 0, 0, 512)
+        cast_pairs(nc.scalar.copy, 1, 0, 256)
+        cast_pairs(nc.vector.tensor_copy, 1, 256, 512)
+        zp_picked = keep.tile([P, S], F32, name="zp_picked")
+        nc.vector.tensor_copy(zp_picked[:], zp_row.indirect(offsets[:]))
+        nc.vector.tensor_copy(picked[:, 0, :], pairs[0].bitcast(U32).indirect(offsets[:]))
+        cast_pairs(nc.scalar.copy, 2, 0, 384)
+        cast_pairs(nc.scalar.copy, 3, 0, 384)
+        cast_pairs(nc.scalar.copy, 4, 0, 256)
+        for g in range(2):
+            nc.vector.tensor_copy(picked[:, 1, 256 * g:256 * (g + 1)],
+                                  pairs[1].bitcast(U32).indirect(offsets[:, 16 * g:16 * (g + 1)]))
+
+        x_grouped = keep.tile([P, S * PACK], BF16, name="x_grouped", align_bytes=64)
+
+        def weave(copy, word, lo, hi):
+            copy(out=x_grouped[:, PACK * lo:PACK * hi].bitcast(word).rearrange("p (n a) -> p n a", a=2),
+                 in_=picked[:, :, lo:hi].bitcast(word).rearrange("p a n -> p n a"))
+
+        weave(nc.vector.tensor_copy, I32, 0, 2 * CHUNK)
+        x_codes = [keep.tile([P, 2 * CHUNK], U32, name=f"x_codes{g}", align_bytes=64) for g in range(2)]
+        x_scales = [keep.tile([P, 2 * CHUNK], U8, name=f"x_scales{g}", align_bytes=64) for g in range(2)]
+
+        def quantize(codes, scales, grouped, lo, hi):
+            nc.vector.quantize_mx(out=codes.bitcast(FP8X4), scales=scales, in_=grouped[:, PACK * lo:PACK * hi])
+
+
+        w_dealt = w_grouped.rearrange("p (t m j) -> p m j t", t=PACK, j=PACK)
+
+        def cast_w(copy, h, lo, hi):
+            copy(out=w_dealt[:, h * 64 + lo:h * 64 + hi, :, :],
+                 in_=w_raw[h][:, :, PACK * lo:PACK * hi].rearrange("p j (m t) -> p m j t", t=PACK))
+
+        cast_w(nc.scalar.copy, 0, 0, 64)
+        cast_w(nc.scalar.copy, 1, 0, 16)
+        cast_w(nc.vector.tensor_copy, 1, 16, 64)
+        weave(nc.scalar.copy, U32, 2 * CHUNK, S)
+        quantize(x_codes[0][:], x_scales[0][:], x_grouped, 0, 2 * CHUNK)
+        w_codes = [keep.tile([P, P], U32, name=f"w_codes{t}", align_bytes=64) for t in range(PACK)]
+        w_scales = [keep.tile([P, P], U8, name=f"w_scales{t}", align_bytes=64) for t in range(PACK)]
+        for t in range(PACK):
+            quantize(w_codes[t][:], w_scales[t][:], w_grouped, t * P, (t + 1) * P)
+        quantize(x_codes[1][:], x_scales[1][:], x_grouped, 2 * CHUNK, S)
+
+        y_rows = out_0.rearrange("(p t) c -> p t c", t=PACK)
+        y_words = out_1.rearrange("z l c r -> (z l) (c r)").bitcast(I32)
+        y_scale_rows = out_2.rearrange("z q c -> (z q) c").bitcast(I32)
+        y_grouped = keep.tile([P, S * PACK], BF16, name="y_grouped", align_bytes=64)
+        y_codes = keep.tile([P, S], U32, name="y_codes", align_bytes=64)
+        y_scales = keep.tile([P, S], U8, name="y_scales", align_bytes=64)
+
+        banks = []
+        for c in range(CHUNKS):
+            cols = slice(c % 2 * CHUNK, (c % 2 + 1) * CHUNK)
+            bank = psum.tile([P, PACK, CHUNK], F32, name=f"y_bank{c}")
+            banks.append(bank)
+            for t in range(PACK):
+                nc.tensor.matmul_mx(out=bank[:, t, :], lhsT=w_codes[t][:].bitcast(FP8X4), lhsT_scale=w_scales[t][:],
+                                    rhs=x_codes[c // 2][:, cols].bitcast(FP8X4), rhs_scale=x_scales[c // 2][:, cols],
+                                    start=True, stop=True)
+
+        y = [keep.tile([P, PACK, CHUNK], F32, name=f"y{c}") for c in range(CHUNKS)]
+
+        def correct(c):
+            cols = slice(c * CHUNK, (c + 1) * CHUNK)
+            for t in range(PACK):
+                nc.vector.scalar_tensor_tensor(y[c][:, t, :], zp_picked[:, cols], neg_csum[:, t:t + 1], banks[c][:, t, :], MULT, ADD)
+            nc.sync.dma_start(out=y_rows[:, :, cols], in_=y[c][:])
+
+        def round_y(copy, c):
+            copy(out=y_grouped[:, PACK * c * CHUNK:PACK * (c + 1) * CHUNK].rearrange("p (n i t) -> p n t i", i=4, t=PACK),
+                 in_=y[c][:].rearrange("p t (n i) -> p n t i", i=4))
+
+        def quantize_y(c):
+            cols = slice(c * CHUNK, (c + 1) * CHUNK)
+            quantize(y_codes[:, cols], y_scales[:, cols], y_grouped, cols.start, cols.stop)
+
+        for c in range(CHUNKS):
+            correct(c)
+            round_y(nc.scalar.copy if c < CHUNKS - 1 else nc.vector.tensor_copy, c)
+            if c > 0:
+                quantize_y(c - 1)
+        nc.scalar.dma_start(out=y_words[:, 0:S - CHUNK], in_=y_codes[:, 0:S - CHUNK].bitcast(I32))
+        quantize_y(CHUNKS - 1)
+        nc.sync.dma_start(out=y_words[:, S - CHUNK:S], in_=y_codes[:, S - CHUNK:S].bitcast(I32))
+        for q in range(4):
+            queue = nc.scalar if q % 2 == 0 else nc.sync
+            queue.dma_start(out=y_scale_rows[4 * q:4 * q + 4, :], in_=y_scales[32 * q:32 * q + 4, :].bitcast(I32))

@@ -33,11 +33,11 @@ def tile_picked_zeropt_none_lo_kernel(tc, xT, zp, csum, w1, offs, out_0, out_1, 
         w_rows = w1.rearrange("(p j) c -> p j c", j=PACK)
 
         offsets = keep.tile([P, S // 16], U16, name="offsets")
-        stage = keep.tile([P, 8192], BF16, name="stage", align_bytes=64)
+        stage = keep.tile([P, 9216], BF16, name="stage", align_bytes=64)
         w_grouped = stage[:, 0:2048]
         pairs = [stage[:, 4096:6144], stage[:, 2032:4080]]
         zp_cols = stage[:, 6128:6144].bitcast(F32)
-        zp_row = stage[:, 6144:8192].bitcast(F32)
+        zp_row = stage[:, 7168:9216].bitcast(F32)
         picked = stage[:, 6144:8192].bitcast(U32).rearrange("p (a n) -> p a n", a=2)
         csum_cols = keep.tile([P, PACK], F32, name="csum_cols")
         pieces = [(0, 0, 512), (0, 512, 1024), (1, 0, 384), (1, 384, 768), (1, 768, 1024)]
@@ -59,7 +59,7 @@ def tile_picked_zeropt_none_lo_kernel(tc, xT, zp, csum, w1, offs, out_0, out_1, 
         nc.gpsimd.tensor_scalar(neg_csum[:], csum_cols[:], -1.0, 0.0, MULT, ADD)
 
         for h in range(2):
-            zp_bank = psum.tile([P, PACK, P], F32, name=f"zp_bank{h}")
+            zp_bank = psum.tile([P, PACK, P], F32, name=f"zp_bank{h}", tag=f"zp_bank{h}")
             for c in range(PACK):
                 nc.tensor.transpose(zp_bank[:, c, :], zp_cols[:, PACK * h + c:PACK * h + c + 1].to_broadcast([P, P]), ident[:])
             nc.vector.tensor_copy(
@@ -92,29 +92,32 @@ def tile_picked_zeropt_none_lo_kernel(tc, xT, zp, csum, w1, offs, out_0, out_1, 
                  in_=picked[:, :, lo:hi].bitcast(word).rearrange("p a n -> p n a"))
 
         weave(nc.vector.tensor_copy, I32, 0, 2 * CHUNK)
-        x_codes = [keep.tile([P, 2 * CHUNK], U32, name=f"x_codes{g}", align_bytes=64) for g in range(2)]
-        x_scales = [keep.tile([P, 2 * CHUNK], U8, name=f"x_scales{g}", align_bytes=64) for g in range(2)]
+        weave(nc.vector.tensor_copy, I32, 2 * CHUNK, S)
+        x_codes = keep.tile([P, S], U32, name="x_codes", align_bytes=64)
+        x_scales = keep.tile([P, S], U8, name="x_scales", align_bytes=64)
 
         def quantize(codes, scales, grouped, lo, hi):
             nc.vector.quantize_mx(out=codes.bitcast(FP8X4), scales=scales, in_=grouped[:, PACK * lo:PACK * hi])
 
 
-        w_dealt = w_grouped.rearrange("p (t m j) -> p m j t", t=PACK, j=PACK)
+        w_dealt = w_grouped.rearrange("p (t m j) -> p m t j", t=PACK, j=PACK)
 
         def cast_w(copy, h, lo, hi):
             copy(out=w_dealt[:, h * 64 + lo:h * 64 + hi, :, :],
-                 in_=w_raw[h][:, :, PACK * lo:PACK * hi].rearrange("p j (m t) -> p m j t", t=PACK))
+                 in_=w_raw[h][:, :, PACK * lo:PACK * hi].rearrange("p j (m t) -> p m t j", t=PACK))
 
         cast_w(nc.scalar.copy, 0, 0, 64)
-        cast_w(nc.scalar.copy, 1, 0, 16)
-        cast_w(nc.vector.tensor_copy, 1, 16, 64)
-        weave(nc.scalar.copy, U32, 2 * CHUNK, S)
-        quantize(x_codes[0][:], x_scales[0][:], x_grouped, 0, 2 * CHUNK)
+        cast_w(nc.scalar.copy, 1, 0, 48)
+        cast_w(nc.vector.tensor_copy, 1, 48, 64)
+
+        def quantize_x(lo, hi):
+            quantize(x_codes[:, lo:hi], x_scales[:, lo:hi], x_grouped, lo, hi)
+
+        quantize_x(0, 2 * CHUNK)
         w_codes = [keep.tile([P, P], U32, name=f"w_codes{t}", align_bytes=64) for t in range(PACK)]
         w_scales = [keep.tile([P, P], U8, name=f"w_scales{t}", align_bytes=64) for t in range(PACK)]
         for t in range(PACK):
             quantize(w_codes[t][:], w_scales[t][:], w_grouped, t * P, (t + 1) * P)
-        quantize(x_codes[1][:], x_scales[1][:], x_grouped, 2 * CHUNK, S)
 
         y_rows = out_0.rearrange("(p t) c -> p t c", t=PACK)
         y_words = out_1.rearrange("z l c r -> (z l) (c r)").bitcast(I32)
@@ -123,14 +126,15 @@ def tile_picked_zeropt_none_lo_kernel(tc, xT, zp, csum, w1, offs, out_0, out_1, 
         y_codes = keep.tile([P, S], U32, name="y_codes", align_bytes=64)
         y_scales = keep.tile([P, S], U8, name="y_scales", align_bytes=64)
 
-        banks = []
-        for c in range(CHUNKS):
-            cols = slice(c % 2 * CHUNK, (c % 2 + 1) * CHUNK)
-            bank = psum.tile([P, PACK, CHUNK], F32, name=f"y_bank{c}")
-            banks.append(bank)
+        first = [psum.tile([P, CHUNK], F32, name=f"first{t}", tag=f"zp_bank{t}") for t in range(PACK)]
+        later = [psum.tile([P, PACK, CHUNK], F32, name=f"y_bank{c}") for c in range(1, CHUNKS)]
+        sums = [[bank[:] for bank in first]] + [[bank[:, t, :] for t in range(PACK)] for bank in later]
+
+        def multiply(c):
+            cols = slice(c * CHUNK, (c + 1) * CHUNK)
             for t in range(PACK):
-                nc.tensor.matmul_mx(out=bank[:, t, :], lhsT=w_codes[t][:].bitcast(FP8X4), lhsT_scale=w_scales[t][:],
-                                    rhs=x_codes[c // 2][:, cols].bitcast(FP8X4), rhs_scale=x_scales[c // 2][:, cols],
+                nc.tensor.matmul_mx(out=sums[c][t], lhsT=w_codes[t][:].bitcast(FP8X4), lhsT_scale=w_scales[t][:],
+                                    rhs=x_codes[:, cols].bitcast(FP8X4), rhs_scale=x_scales[:, cols],
                                     start=True, stop=True)
 
         y = [keep.tile([P, PACK, CHUNK], F32, name=f"y{c}") for c in range(CHUNKS)]
@@ -138,7 +142,7 @@ def tile_picked_zeropt_none_lo_kernel(tc, xT, zp, csum, w1, offs, out_0, out_1, 
         def correct(c):
             cols = slice(c * CHUNK, (c + 1) * CHUNK)
             for t in range(PACK):
-                nc.vector.scalar_tensor_tensor(y[c][:, t, :], zp_picked[:, cols], neg_csum[:, t:t + 1], banks[c][:, t, :], MULT, ADD)
+                nc.vector.scalar_tensor_tensor(y[c][:, t, :], zp_picked[:, cols], neg_csum[:, t:t + 1], sums[c][t], MULT, ADD)
             nc.sync.dma_start(out=y_rows[:, :, cols], in_=y[c][:])
 
         def round_y(copy, c):
@@ -149,8 +153,14 @@ def tile_picked_zeropt_none_lo_kernel(tc, xT, zp, csum, w1, offs, out_0, out_1, 
             cols = slice(c * CHUNK, (c + 1) * CHUNK)
             quantize(y_codes[:, cols], y_scales[:, cols], y_grouped, cols.start, cols.stop)
 
+        multiply(0)
+        multiply(1)
         for c in range(CHUNKS):
             correct(c)
+            if c == 0:
+                quantize_x(2 * CHUNK, S)
+                multiply(2)
+                multiply(3)
             round_y(nc.scalar.copy if c < CHUNKS - 1 else nc.vector.tensor_copy, c)
             if c > 0:
                 quantize_y(c - 1)

@@ -33,12 +33,12 @@ def tile_picked_zeropt_none_lo_kernel(tc, xT, zp, csum, w1, offs, out_0, out_1, 
         w_rows = w1.rearrange("(p j) c -> p j c", j=PACK)
 
         offsets = keep.tile([P, S // 16], U16, name="offsets")
-        stage = keep.tile([P, 9216], BF16, name="stage", align_bytes=64)
+        stage = keep.tile([P, 10208], BF16, name="stage", align_bytes=64)
         w_grouped = stage[:, 0:2048]
-        pairs = [stage[:, 4096:6144], stage[:, 2032:4080]]
-        zp_cols = stage[:, 6128:6144].bitcast(F32)
-        zp_row = stage[:, 7168:9216].bitcast(F32)
-        picked = stage[:, 6144:8192].bitcast(U32).rearrange("p (a n) -> p a n", a=2)
+        pairs = [stage[:, 6112:8160], stage[:, 2032:4080]]
+        zp_cols = stage[:, 8144:8160].bitcast(F32)
+        zp_row = stage[:, 4064:6112].bitcast(F32)
+        picked = stage[:, 8160:10208].bitcast(U32).rearrange("p (a n) -> p a n", a=2)
         csum_cols = keep.tile([P, PACK], F32, name="csum_cols")
         pieces = [(0, 0, 512), (0, 512, 1024), (1, 0, 384), (1, 384, 768), (1, 768, 1024)]
         x_raw = [keep.tile([P, 2, hi - lo], F32, name=f"x_raw{i}") for i, (a, lo, hi) in enumerate(pieces)]
@@ -80,7 +80,8 @@ def tile_picked_zeropt_none_lo_kernel(tc, xT, zp, csum, w1, offs, out_0, out_1, 
         nc.vector.tensor_copy(picked[:, 0, :], pairs[0].bitcast(U32).indirect(offsets[:]))
         cast_pairs(nc.scalar.copy, 2, 0, 384)
         cast_pairs(nc.scalar.copy, 3, 0, 384)
-        cast_pairs(nc.scalar.copy, 4, 0, 256)
+        cast_pairs(nc.scalar.copy, 4, 0, 128)
+        cast_pairs(nc.vector.tensor_copy, 4, 128, 256)
         for g in range(2):
             nc.vector.tensor_copy(picked[:, 1, 256 * g:256 * (g + 1)],
                                   pairs[1].bitcast(U32).indirect(offsets[:, 16 * g:16 * (g + 1)]))
@@ -92,7 +93,6 @@ def tile_picked_zeropt_none_lo_kernel(tc, xT, zp, csum, w1, offs, out_0, out_1, 
                  in_=picked[:, :, lo:hi].bitcast(word).rearrange("p a n -> p n a"))
 
         weave(nc.vector.tensor_copy, I32, 0, 2 * CHUNK)
-        weave(nc.vector.tensor_copy, I32, 2 * CHUNK, S)
         x_codes = keep.tile([P, S], U32, name="x_codes", align_bytes=64)
         x_scales = keep.tile([P, S], U8, name="x_scales", align_bytes=64)
 
@@ -100,15 +100,16 @@ def tile_picked_zeropt_none_lo_kernel(tc, xT, zp, csum, w1, offs, out_0, out_1, 
             nc.vector.quantize_mx(out=codes.bitcast(FP8X4), scales=scales, in_=grouped[:, PACK * lo:PACK * hi])
 
 
-        w_dealt = w_grouped.rearrange("p (t m j) -> p m t j", t=PACK, j=PACK)
+        w_dealt = w_grouped.rearrange("p (t m j) -> p m j t", t=PACK, j=PACK)
 
         def cast_w(copy, h, lo, hi):
             copy(out=w_dealt[:, h * 64 + lo:h * 64 + hi, :, :],
-                 in_=w_raw[h][:, :, PACK * lo:PACK * hi].rearrange("p j (m t) -> p m t j", t=PACK))
+                 in_=w_raw[h][:, :, PACK * lo:PACK * hi].rearrange("p j (m t) -> p m j t", t=PACK))
 
         cast_w(nc.scalar.copy, 0, 0, 64)
-        cast_w(nc.scalar.copy, 1, 0, 48)
-        cast_w(nc.vector.tensor_copy, 1, 48, 64)
+        cast_w(nc.scalar.copy, 1, 0, 16)
+        cast_w(nc.vector.tensor_copy, 1, 16, 64)
+        weave(nc.scalar.copy, U32, 2 * CHUNK, S)
 
         def quantize_x(lo, hi):
             quantize(x_codes[:, lo:hi], x_scales[:, lo:hi], x_grouped, lo, hi)
@@ -118,6 +119,8 @@ def tile_picked_zeropt_none_lo_kernel(tc, xT, zp, csum, w1, offs, out_0, out_1, 
         w_scales = [keep.tile([P, P], U8, name=f"w_scales{t}", align_bytes=64) for t in range(PACK)]
         for t in range(PACK):
             quantize(w_codes[t][:], w_scales[t][:], w_grouped, t * P, (t + 1) * P)
+
+        quantize_x(2 * CHUNK, S)
 
         y_rows = out_0.rearrange("(p t) c -> p t c", t=PACK)
         y_words = out_1.rearrange("z l c r -> (z l) (c r)").bitcast(I32)
@@ -145,25 +148,22 @@ def tile_picked_zeropt_none_lo_kernel(tc, xT, zp, csum, w1, offs, out_0, out_1, 
                 nc.vector.scalar_tensor_tensor(y[c][:, t, :], zp_picked[:, cols], neg_csum[:, t:t + 1], sums[c][t], MULT, ADD)
             nc.sync.dma_start(out=y_rows[:, :, cols], in_=y[c][:])
 
-        def round_y(copy, c):
-            copy(out=y_grouped[:, PACK * c * CHUNK:PACK * (c + 1) * CHUNK].rearrange("p (n i t) -> p n t i", i=4, t=PACK),
-                 in_=y[c][:].rearrange("p t (n i) -> p n t i", i=4))
+        def round_y(copy, c, lo, hi):
+            copy(out=y_grouped[:, PACK * (c * CHUNK + lo):PACK * (c * CHUNK + hi)].rearrange("p (n i t) -> p n t i", i=4, t=PACK),
+                 in_=y[c][:, :, lo:hi].rearrange("p t (n i) -> p n t i", i=4))
 
         def quantize_y(c):
             cols = slice(c * CHUNK, (c + 1) * CHUNK)
             quantize(y_codes[:, cols], y_scales[:, cols], y_grouped, cols.start, cols.stop)
 
-        multiply(0)
-        multiply(1)
+        for c in range(CHUNKS):
+            multiply(c)
         for c in range(CHUNKS):
             correct(c)
-            if c == 0:
-                quantize_x(2 * CHUNK, S)
-                multiply(2)
-                multiply(3)
-            round_y(nc.scalar.copy if c < CHUNKS - 1 else nc.vector.tensor_copy, c)
+            round_y(nc.scalar.copy, c, 0, CHUNK if c < CHUNKS - 1 else 48)
             if c > 0:
                 quantize_y(c - 1)
+        round_y(nc.vector.tensor_copy, CHUNKS - 1, 48, CHUNK)
         nc.scalar.dma_start(out=y_words[:, 0:S - CHUNK], in_=y_codes[:, 0:S - CHUNK].bitcast(I32))
         quantize_y(CHUNKS - 1)
         nc.sync.dma_start(out=y_words[:, S - CHUNK:S], in_=y_codes[:, S - CHUNK:S].bitcast(I32))

@@ -33,14 +33,14 @@ def tile_picked_zeropt_none_lo_kernel(tc, xT, zp, csum, w1, offs, out_0, out_1, 
         w_rows = w1.rearrange("(p j) c -> p j c", j=PACK)
 
         offsets = keep.tile([P, S // 16], U16, name="offsets")
-        stage = keep.tile([P, 10208], BF16, name="stage", align_bytes=64)
+        stage = keep.tile([P, 9216], BF16, name="stage", align_bytes=64)
         w_grouped = stage[:, 0:2048]
-        pairs = [stage[:, 6112:8160], stage[:, 2032:4080]]
-        zp_cols = stage[:, 8144:8160].bitcast(F32)
-        zp_row = stage[:, 4064:6112].bitcast(F32)
-        picked = stage[:, 8160:10208].bitcast(U32).rearrange("p (a n) -> p a n", a=2)
+        pairs = [stage[:, 4096:6144], stage[:, 2032:4080]]
+        zp_cols = stage[:, 6128:6144].bitcast(F32)
+        zp_row = stage[:, 7168:9216].bitcast(F32)
+        picked = stage[:, 6144:8192].bitcast(U32).rearrange("p (a n) -> p a n", a=2)
         csum_cols = keep.tile([P, PACK], F32, name="csum_cols")
-        pieces = [(0, 0, 512), (0, 512, 1024), (1, 0, 384), (1, 384, 768), (1, 768, 1024)]
+        pieces = [(0, 0, 512), (0, 512, 1024), (1, 0, 256), (1, 256, 512), (1, 512, 768), (1, 768, 1024)]
         x_raw = [keep.tile([P, 2, hi - lo], F32, name=f"x_raw{i}") for i, (a, lo, hi) in enumerate(pieces)]
         w_raw = [keep.tile([P, PACK, N // 2], F32, name=f"w_raw{h}") for h in range(2)]
 
@@ -59,7 +59,7 @@ def tile_picked_zeropt_none_lo_kernel(tc, xT, zp, csum, w1, offs, out_0, out_1, 
         nc.gpsimd.tensor_scalar(neg_csum[:], csum_cols[:], -1.0, 0.0, MULT, ADD)
 
         for h in range(2):
-            zp_bank = psum.tile([P, PACK, P], F32, name=f"zp_bank{h}", tag=f"zp_bank{h}")
+            zp_bank = psum.tile([P, PACK, P], F32, name=f"zp_bank{h}")
             for c in range(PACK):
                 nc.tensor.transpose(zp_bank[:, c, :], zp_cols[:, PACK * h + c:PACK * h + c + 1].to_broadcast([P, P]), ident[:])
             nc.vector.tensor_copy(
@@ -78,10 +78,8 @@ def tile_picked_zeropt_none_lo_kernel(tc, xT, zp, csum, w1, offs, out_0, out_1, 
         zp_picked = keep.tile([P, S], F32, name="zp_picked")
         nc.vector.tensor_copy(zp_picked[:], zp_row.indirect(offsets[:]))
         nc.vector.tensor_copy(picked[:, 0, :], pairs[0].bitcast(U32).indirect(offsets[:]))
-        cast_pairs(nc.scalar.copy, 2, 0, 384)
-        cast_pairs(nc.scalar.copy, 3, 0, 384)
-        cast_pairs(nc.scalar.copy, 4, 0, 128)
-        cast_pairs(nc.vector.tensor_copy, 4, 128, 256)
+        for i in range(2, 6):
+            cast_pairs(nc.scalar.copy, i, 0, 256)
         for g in range(2):
             nc.vector.tensor_copy(picked[:, 1, 256 * g:256 * (g + 1)],
                                   pairs[1].bitcast(U32).indirect(offsets[:, 16 * g:16 * (g + 1)]))
@@ -129,14 +127,11 @@ def tile_picked_zeropt_none_lo_kernel(tc, xT, zp, csum, w1, offs, out_0, out_1, 
         y_codes = keep.tile([P, S], U32, name="y_codes", align_bytes=64)
         y_scales = keep.tile([P, S], U8, name="y_scales", align_bytes=64)
 
-        first = [psum.tile([P, CHUNK], F32, name=f"first{t}", tag=f"zp_bank{t}") for t in range(PACK)]
-        later = [psum.tile([P, PACK, CHUNK], F32, name=f"y_bank{c}") for c in range(1, CHUNKS)]
-        sums = [[bank[:] for bank in first]] + [[bank[:, t, :] for t in range(PACK)] for bank in later]
-
-        def multiply(c):
+        banks = [psum.tile([P, PACK, CHUNK], F32, name=f"y_bank{c}") for c in range(CHUNKS)]
+        for c in range(CHUNKS):
             cols = slice(c * CHUNK, (c + 1) * CHUNK)
             for t in range(PACK):
-                nc.tensor.matmul_mx(out=sums[c][t], lhsT=w_codes[t][:].bitcast(FP8X4), lhsT_scale=w_scales[t][:],
+                nc.tensor.matmul_mx(out=banks[c][:, t, :], lhsT=w_codes[t][:].bitcast(FP8X4), lhsT_scale=w_scales[t][:],
                                     rhs=x_codes[:, cols].bitcast(FP8X4), rhs_scale=x_scales[:, cols],
                                     start=True, stop=True)
 
@@ -145,27 +140,25 @@ def tile_picked_zeropt_none_lo_kernel(tc, xT, zp, csum, w1, offs, out_0, out_1, 
         def correct(c):
             cols = slice(c * CHUNK, (c + 1) * CHUNK)
             for t in range(PACK):
-                nc.vector.scalar_tensor_tensor(y[c][:, t, :], zp_picked[:, cols], neg_csum[:, t:t + 1], sums[c][t], MULT, ADD)
+                nc.vector.scalar_tensor_tensor(y[c][:, t, :], zp_picked[:, cols], neg_csum[:, t:t + 1], banks[c][:, t, :], MULT, ADD)
             nc.sync.dma_start(out=y_rows[:, :, cols], in_=y[c][:])
 
-        def round_y(copy, c, lo, hi):
-            copy(out=y_grouped[:, PACK * (c * CHUNK + lo):PACK * (c * CHUNK + hi)].rearrange("p (n i t) -> p n t i", i=4, t=PACK),
-                 in_=y[c][:, :, lo:hi].rearrange("p t (n i) -> p n t i", i=4))
+        def round_y(copy, c):
+            copy(out=y_grouped[:, PACK * c * CHUNK:PACK * (c + 1) * CHUNK].rearrange("p (n i t) -> p n t i", i=4, t=PACK),
+                 in_=y[c][:].rearrange("p t (n i) -> p n t i", i=4))
 
-        def quantize_y(c):
-            cols = slice(c * CHUNK, (c + 1) * CHUNK)
-            quantize(y_codes[:, cols], y_scales[:, cols], y_grouped, cols.start, cols.stop)
+        def quantize_y(lo, hi):
+            quantize(y_codes[:, lo:hi], y_scales[:, lo:hi], y_grouped, lo, hi)
 
-        for c in range(CHUNKS):
-            multiply(c)
-        for c in range(CHUNKS):
+        for c in range(CHUNKS - 1):
             correct(c)
-            round_y(nc.scalar.copy, c, 0, CHUNK if c < CHUNKS - 1 else 48)
-            if c > 0:
-                quantize_y(c - 1)
-        round_y(nc.vector.tensor_copy, CHUNKS - 1, 48, CHUNK)
+            round_y(nc.scalar.copy, c)
+        quantize_y(0, 2 * CHUNK)
+        correct(CHUNKS - 1)
+        quantize_y(2 * CHUNK, 3 * CHUNK)
         nc.scalar.dma_start(out=y_words[:, 0:S - CHUNK], in_=y_codes[:, 0:S - CHUNK].bitcast(I32))
-        quantize_y(CHUNKS - 1)
+        round_y(nc.vector.tensor_copy, CHUNKS - 1)
+        quantize_y(3 * CHUNK, S)
         nc.sync.dma_start(out=y_words[:, S - CHUNK:S], in_=y_codes[:, S - CHUNK:S].bitcast(I32))
         for q in range(4):
             queue = nc.scalar if q % 2 == 0 else nc.sync

from contextlib import ExitStack

import concourse.mybir as mybir
from concourse.masks import make_identity

K, T, S, N = 512, 1024, 512, 512
FLOPS = 2 * K * S * N

F32 = mybir.dt.float32
BF16 = mybir.dt.bfloat16
I32 = mybir.dt.int32
U32 = mybir.dt.uint32
U16 = mybir.dt.uint16
U8 = mybir.dt.uint8
FP8X4 = mybir.dt.float8_e4m3fn_x4
MULT = mybir.AluOpType.mult
ADD = mybir.AluOpType.add

P = 128
PACK = 4
HALF = T // 2
CHUNK = 128
CHUNKS = S // CHUNK


def tile_picked_zeropt_none_lo_kernel(tc, xT, zp, csum, w1, offs, out_0, out_1, out_2):
    nc = tc.nc
    with ExitStack() as ctx:
        keep = ctx.enter_context(tc.tile_pool(name="keep", bufs=1))
        psum = ctx.enter_context(tc.psum_pool(name="psum", bufs=1))

        x_rows = xT.rearrange("(p j) c -> p j c", j=PACK)
        w_rows = w1.rearrange("(p j) c -> p j c", j=PACK)

        offsets = keep.tile([P, S // 16], U16, name="offsets")
        stage = keep.tile([P, 9216], BF16, name="stage", align_bytes=64)
        w_grouped = stage[:, 0:2048]
        pairs = [stage[:, 4096:6144], stage[:, 2032:4080]]
        zp_cols = stage[:, 6128:6144].bitcast(F32)
        zp_row = stage[:, 7168:9216].bitcast(F32)
        picked = stage[:, 6144:8192].bitcast(U32).rearrange("p (a n) -> p a n", a=2)
        csum_cols = keep.tile([P, PACK], F32, name="csum_cols")
        pieces = [(0, 0, 512), (0, 512, 1024), (1, 0, 256), (1, 256, 512), (1, 512, 768), (1, 768, 1024)]
        x_raw = [keep.tile([P, 2, hi - lo], F32, name=f"x_raw{i}") for i, (a, lo, hi) in enumerate(pieces)]
        w_raw = [keep.tile([P, PACK, N // 2], F32, name=f"w_raw{h}") for h in range(2)]

        nc.sync.dma_start(out=zp_cols, in_=zp[0:1, :].rearrange("o (p c) -> (o p) c", c=2 * PACK))
        nc.scalar.dma_start(out=csum_cols[:], in_=csum.rearrange("(p t) o -> p (t o)", t=PACK))
        for i, (a, lo, hi) in enumerate(pieces):
            nc.sync.dma_start(out=x_raw[i][:], in_=x_rows[:, 2 * a:2 * a + 2, lo:hi])
            if i == 0:
                nc.sync.dma_start(offsets[:], offs)
        for h in range(2):
            nc.sync.dma_start(out=w_raw[h][:], in_=w_rows[:, :, h * (N // 2):(h + 1) * (N // 2)])

        ident = keep.tile([P, P], F32, name="ident")
        make_identity(nc, ident[:])
        neg_csum = keep.tile([P, PACK], F32, name="neg_csum")
        nc.gpsimd.tensor_scalar(neg_csum[:], csum_cols[:], -1.0, 0.0, MULT, ADD)

        for h in range(2):
            zp_bank = psum.tile([P, PACK, P], F32, name=f"zp_bank{h}")
            for c in range(PACK):
                nc.tensor.transpose(zp_bank[:, c, :], zp_cols[:, PACK * h + c:PACK * h + c + 1].to_broadcast([P, P]), ident[:])
            nc.vector.tensor_copy(
                out=zp_row.rearrange("p (n h c) -> p h n c", h=2, c=PACK)[:, h, :, :],
                in_=zp_bank[:].rearrange("p c n -> p n c"))


        def cast_pairs(copy, i, lo, hi):
            a, first, last = pieces[i]
            copy(out=pairs[a][:, 2 * (first + lo):2 * (first + hi)].rearrange("p (n j) -> p n j", j=2),
                 in_=x_raw[i][:, :, lo:hi].rearrange("p j n -> p n j"))

        cast_pairs(nc.scalar.copy, 0, 0, 512)
        cast_pairs(nc.scalar.copy, 1, 0, 256)
        cast_pairs(nc.vector.tensor_copy, 1, 256, 512)
        zp_picked = keep.tile([P, S], F32, name="zp_picked")
        nc.vector.tensor_copy(zp_picked[:], zp_row.indirect(offsets[:]))
        nc.vector.tensor_copy(picked[:, 0, :], pairs[0].bitcast(U32).indirect(offsets[:]))
        for i in range(2, 6):
            cast_pairs(nc.scalar.copy, i, 0, 256)
        for g in range(2):
            nc.vector.tensor_copy(picked[:, 1, 256 * g:256 * (g + 1)],
                                  pairs[1].bitcast(U32).indirect(offsets[:, 16 * g:16 * (g + 1)]))

        x_grouped = keep.tile([P, S * PACK], BF16, name="x_grouped", align_bytes=64)

        def weave(copy, word, lo, hi):
            copy(out=x_grouped[:, PACK * lo:PACK * hi].bitcast(word).rearrange("p (n a) -> p n a", a=2),
                 in_=picked[:, :, lo:hi].bitcast(word).rearrange("p a n -> p n a"))

        weave(nc.vector.tensor_copy, I32, 0, 2 * CHUNK)
        x_codes = keep.tile([P, S], U32, name="x_codes", align_bytes=64)
        x_scales = keep.tile([P, S], U8, name="x_scales", align_bytes=64)

        def quantize(codes, scales, grouped, lo, hi):
            nc.vector.quantize_mx(out=codes.bitcast(FP8X4), scales=scales, in_=grouped[:, PACK * lo:PACK * hi])


        w_dealt = w_grouped.rearrange("p (t m j) -> p m j t", t=PACK, j=PACK)

        def cast_w(copy, h, lo, hi):
            copy(out=w_dealt[:, h * 64 + lo:h * 64 + hi, :, :],
                 in_=w_raw[h][:, :, PACK * lo:PACK * hi].rearrange("p j (m t) -> p m j t", t=PACK))

        cast_w(nc.scalar.copy, 0, 0, 64)
        cast_w(nc.scalar.copy, 1, 0, 16)
        cast_w(nc.vector.tensor_copy, 1, 16, 64)
        weave(nc.scalar.copy, U32, 2 * CHUNK, S)

        def quantize_x(lo, hi):
            quantize(x_codes[:, lo:hi], x_scales[:, lo:hi], x_grouped, lo, hi)

        quantize_x(0, 2 * CHUNK)
        w_codes = [keep.tile([P, P], U32, name=f"w_codes{t}", align_bytes=64) for t in range(PACK)]
        w_scales = [keep.tile([P, P], U8, name=f"w_scales{t}", align_bytes=64) for t in range(PACK)]
        for t in range(PACK):
            quantize(w_codes[t][:], w_scales[t][:], w_grouped, t * P, (t + 1) * P)

        quantize_x(2 * CHUNK, S)

        y_rows = out_0.rearrange("(p t) c -> p t c", t=PACK)
        y_words = out_1.rearrange("z l c r -> (z l) (c r)").bitcast(I32)
        y_scale_rows = out_2.rearrange("z q c -> (z q) c").bitcast(I32)
        y_grouped = keep.tile([P, S * PACK], BF16, name="y_grouped", align_bytes=64)
        y_codes = keep.tile([P, S], U32, name="y_codes", align_bytes=64)
        y_scales = keep.tile([P, S], U8, name="y_scales", align_bytes=64)

        banks = [psum.tile([P, PACK, CHUNK], F32, name=f"y_bank{c}") for c in range(CHUNKS)]
        for c in range(CHUNKS):
            cols = slice(c * CHUNK, (c + 1) * CHUNK)
            for t in range(PACK):
                nc.tensor.matmul_mx(out=banks[c][:, t, :], lhsT=w_codes[t][:].bitcast(FP8X4), lhsT_scale=w_scales[t][:],
                                    rhs=x_codes[:, cols].bitcast(FP8X4), rhs_scale=x_scales[:, cols],
                                    start=True, stop=True)

        y = [keep.tile([P, PACK, CHUNK], F32, name=f"y{c}") for c in range(CHUNKS)]

        def correct(c):
            cols = slice(c * CHUNK, (c + 1) * CHUNK)
            for t in range(PACK):
                nc.vector.scalar_tensor_tensor(y[c][:, t, :], zp_picked[:, cols], neg_csum[:, t:t + 1], banks[c][:, t, :], MULT, ADD)
            nc.sync.dma_start(out=y_rows[:, :, cols], in_=y[c][:])

        def round_y(copy, c):
            copy(out=y_grouped[:, PACK * c * CHUNK:PACK * (c + 1) * CHUNK].rearrange("p (n i t) -> p n t i", i=4, t=PACK),
                 in_=y[c][:].rearrange("p t (n i) -> p n t i", i=4))

        def quantize_y(lo, hi):
            quantize(y_codes[:, lo:hi], y_scales[:, lo:hi], y_grouped, lo, hi)

        for c in range(CHUNKS - 1):
            correct(c)
            round_y(nc.scalar.copy, c)
        quantize_y(0, 2 * CHUNK)
        correct(CHUNKS - 1)
        quantize_y(2 * CHUNK, 3 * CHUNK)
        nc.scalar.dma_start(out=y_words[:, 0:S - CHUNK], in_=y_codes[:, 0:S - CHUNK].bitcast(I32))
        round_y(nc.vector.tensor_copy, CHUNKS - 1)
        quantize_y(3 * CHUNK, S)
        nc.sync.dma_start(out=y_words[:, S - CHUNK:S], in_=y_codes[:, S - CHUNK:S].bitcast(I32))
        for q in range(4):
            queue = nc.scalar if q % 2 == 0 else nc.sync
            queue.dma_start(out=y_scale_rows[4 * q:4 * q + 4, :], in_=y_scales[32 * q:32 * q + 4, :].bitcast(I32))
